import numpy as np
import ml_dtypes


def mxq(x, axis, fmt="e4m3"):
    dtype, down = {"e4m3": (ml_dtypes.float8_e4m3fn, 7), "e5m2": (ml_dtypes.float8_e5m2, 14)}[fmt]
    v = np.moveaxis(np.asarray(x, np.float32).astype(ml_dtypes.bfloat16).astype(np.float64), axis, -1)
    blocks = v.reshape(v.shape[:-1] + (-1, 32))
    amax = np.abs(blocks).max(-1, keepdims=True)
    byte = np.maximum(np.where(amax > 0, np.frexp(amax)[1] - 1 + 127, 0) - down, 1)
    scale = np.exp2(byte - 127.0)
    codes = (blocks / scale).astype(np.float32).astype(dtype).astype(np.float64)
    return np.moveaxis((codes * scale).reshape(v.shape), -1, axis)


WIDE = False


def mx_kscale(k):
    if not WIDE:
        return np.ones(k)
    levels = np.array([10, -10, 5, -5, 0])
    if k % 512:
        return np.exp2(np.random.permutation(np.resize(levels, k // 32))).repeat(32)
    a = np.empty((k // 512, 16))
    for p in range(k // 512):
        a[p, :8] = np.random.permutation(np.resize(levels, 8))
        for g in range(8):
            far = levels[np.abs(levels - a[p, g]) >= 10]
            a[p, g + 8] = far[np.random.randint(len(far))]
    return np.exp2(a.ravel()).repeat(32)


def f64(x):
    return np.asarray(x).astype(np.float64)


def striped(idx):
    return np.tile(idx.reshape(-1, 16).T, (8, 1)).astype(np.uint16)


def unstriped(offs):
    return offs[:16].T.reshape(-1).astype(np.int64)


E2M1 = np.array([0.0, 0.5, 1.0, 1.5, 2.0, 3.0, 4.0, 6.0, -0.0, -0.5, -1.0, -1.5, -2.0, -3.0, -4.0, -6.0])


def pack_weight(w, fmt):
    k, n = w.shape
    w = f64(np.asarray(w, np.float32).astype(ml_dtypes.bfloat16)).reshape(k // 32, 32, n)
    amax = np.abs(w).max(1)
    if fmt == "e4m3":
        byte = np.frexp(amax)[1] - 1 + 127 - 7
    else:
        mant, ex = np.frexp(amax / 6.0)
        byte = np.where(mant > 0.5, ex, ex - 1) + 127
    byte = np.clip(np.where(amax > 0, byte, 1), 1, 254)
    scaled = (w * np.exp2(127.0 - byte)[:, None, :]).reshape(k, n).astype(np.float32)
    by_word = np.ascontiguousarray(scaled.reshape(k // 512, 128, 4, n).transpose(0, 1, 3, 2))
    if fmt == "e4m3":
        words = by_word.astype(ml_dtypes.float8_e4m3fn).view(np.uint8)
    else:
        c = by_word.astype(ml_dtypes.float4_e2m1fn).view(np.uint8) & 0xF
        words = (c[..., 0::2] | (c[..., 1::2] << 4)).reshape(k // 512, 128, 2 * n)
    return np.ascontiguousarray(words), np.ascontiguousarray(byte.astype(np.uint8).reshape(k // 512, 16, n))


def unpack_weight(words, scales, fmt):
    g, _, n = scales.shape
    words = np.ascontiguousarray(words).reshape(g, 128, n, -1)
    if fmt == "e4m3":
        vals = words.view(ml_dtypes.float8_e4m3fn).astype(np.float64)
    else:
        nib = np.empty((g, 128, n, 4), np.uint8)
        nib[..., 0::2] = words & 0xF
        nib[..., 1::2] = words >> 4
        vals = E2M1[nib]
    vals = vals * np.repeat(np.exp2(scales.astype(np.float64) - 127.0), 8, axis=1)[..., None]
    return vals.transpose(0, 1, 3, 2).reshape(g * 512, n)


def silu(v):
    return v / (1.0 + np.exp(-np.maximum(v, -700.0)))


K, T, E, C, H, N = 1536, 1024, 2, 256, 512, 384


def by_expert(wq, xq):
    return np.concatenate([wq[e].T @ xq[:, e * C:(e + 1) * C] for e in range(E)], axis=1)


def setup_inputs():
    n = np.random.standard_normal
    s = mx_kscale(K)[:, None]
    u = mx_kscale(H)
    w1 = [pack_weight(m, "e2m1") for m in n((E + 1, K, H)) / np.sqrt(K) / s[None]]
    w3 = [pack_weight(m, "e2m1") for m in n((E + 1, K, H)) / np.sqrt(K) / s[None] * u[None, None, :]]
    w2 = [pack_weight(m, "e2m1") for m in n((E + 1, H, N)) / np.sqrt(H) / u[None, :, None]]
    x = pack_weight(n((K, T)) * s, "e4m3")
    return {
        "x_words": x[0],
        "x_scales": x[1],
        "w1_words": np.stack([m[0] for m in w1]),
        "w1_scales": np.stack([m[1] for m in w1]),
        "w3_words": np.stack([m[0] for m in w3]),
        "w3_scales": np.stack([m[1] for m in w3]),
        "w2_words": np.stack([m[0] for m in w2]),
        "w2_scales": np.stack([m[1] for m in w2]),
        "gate": np.tile(np.random.uniform(0.2, 1.0, E * C), (N, 1)).astype(np.float32),
        "offs": striped(np.random.permutation(T)[:E * C]),
    }


def reference(x_words, x_scales, w1_words, w1_scales, w3_words, w3_scales, w2_words, w2_scales, gate, offs):
    idx = unstriped(offs)
    w1 = np.stack([unpack_weight(w1_words[e], w1_scales[e], "e2m1") for e in range(E + 1)])
    w3 = np.stack([unpack_weight(w3_words[e], w3_scales[e], "e2m1") for e in range(E + 1)])
    w2 = np.stack([unpack_weight(w2_words[e], w2_scales[e], "e2m1") for e in range(E + 1)])
    w1q, w3q, w2q = w1, w3, w2
    xs = unpack_weight(x_words, x_scales, "e4m3")
    hs = silu(w1q[E].T @ xs) * (w3q[E].T @ xs)
    ys = w2q[E].T @ mxq(hs, 0, "e4m3")
    xq = unpack_weight(x_words, x_scales, "e4m3")[:, idx]
    h = silu(by_expert(w1q, xq))
    h = h * by_expert(w3q, xq)
    y = by_expert(w2q, mxq(h, 0, "e4m3"))
    out = ys
    out[:, idx] += f64(gate) * y
    return out

@@ -1,0 +1,239 @@
+from contextlib import ExitStack
+
+import concourse.mybir as mybir
+from concourse.masks import make_identity
+
+K, T, E, C, H, N = 1536, 1024, 2, 256, 512, 384
+FLOPS = 2 * (T + E * C) * (2 * K * H + H * N)
+
+F32 = mybir.dt.float32
+BF16 = mybir.dt.bfloat16
+I32 = mybir.dt.int32
+U32 = mybir.dt.uint32
+U16 = mybir.dt.uint16
+U8 = mybir.dt.uint8
+FP8X4 = mybir.dt.float8_e4m3fn_x4
+FP4X4 = mybir.dt.float4_e2m1fn_x4
+MULT = mybir.AluOpType.mult
+ADD = mybir.AluOpType.add
+SILU = mybir.ActivationFunctionType.Silu
+
+P = 128
+PASSES = K // 512
+SHARED = E
+BLOCKS = N // P
+GROUP = 256
+
+
+def tile_moe_shr_glu_silu_kernel(
+    tc, x_words, x_scales, w1_words, w1_scales, w3_words, w3_scales, w2_words, w2_scales, gate, offs, out
+):
+    nc = tc.nc
+    with ExitStack() as ctx:
+        keep = ctx.enter_context(tc.tile_pool(name="keep", bufs=1))
+        work = ctx.enter_context(tc.tile_pool(name="work", bufs=1))
+        psum = ctx.enter_context(tc.psum_pool(name="psum", bufs=1))
+
+        offsets = keep.tile([P, E * C // 16], U16, name="offsets")
+        xw = [keep.tile([P, T], U32, name="xw%d" % s, align_bytes=64) for s in range(PASSES)]
+        xs = keep.tile([P, PASSES, T], U8, name="xs", align_bytes=64)
+        w1 = [keep.tile([P, PASSES, 2 * H], U8, name="w1_%d" % e, align_bytes=64) for e in range(E + 1)]
+        w3 = [keep.tile([P, PASSES, 2 * H], U8, name="w3_%d" % e, align_bytes=64) for e in range(E + 1)]
+        w2 = keep.tile([P, E + 1, 2 * N], U8, name="w2", align_bytes=64)
+        w1s_shared = keep.tile([P, PASSES, H], U8, name="w1s_shared", align_bytes=64)
+        w1s_routed = keep.tile([P, E * PASSES, H], U8, name="w1s_routed", align_bytes=64)
+        w3s = keep.tile([P, (E + 1) * PASSES, H], U8, name="w3s", align_bytes=64)
+        w2s = keep.tile([P, E + 1, N], U8, name="w2s", align_bytes=64)
+        gate_sb = keep.tile([P, E * C], F32, name="gate_sb")
+        routed = [keep.tile([P, T], F32, name="routed%d" % b) for b in range(BLOCKS)]
+        ident = keep.tile([P, P], F32, name="ident")
+        warm = keep.tile([P, 8], F32, name="warm")
+        banks = [psum.tile([P, 512], F32, name="bank%d" % i) for i in range(8)]
+
+        def load_scales(plane, rows):
+            for r in range(4):
+                nc.sync.dma_start(out=plane[r:P:32].bitcast(I32), in_=rows[:, r:16:4, :].rearrange("s q c -> q s c").bitcast(I32))
+
+        def load_x(s):
+            nc.sync.dma_start(out=xw[s][:].bitcast(I32), in_=x_words[s].rearrange("p t r -> p (t r)").bitcast(I32))
+
+        def load_w(tile, words):
+            nc.sync.dma_start(out=tile[:].bitcast(I32), in_=words.rearrange("s p c -> p s c").bitcast(I32))
+
+        nc.gpsimd.memset(w1s_shared[:].bitcast(I32), 0)
+        for plane in (xs, w3s, w1s_routed, w2s):
+            nc.vector.memset(plane[:].bitcast(I32), 0)
+        make_identity(nc, ident[:])
+        nc.scalar.activation(out=warm[:, 0:1], in_=ident[:, 0:1], func=SILU)
+
+        load_x(0)
+        load_w(w1[SHARED], w1_words[SHARED])
+        nc.sync.dma_start(offsets[:], offs)
+        load_scales(w1s_shared, w1_scales[SHARED])
+        load_scales(xs, x_scales)
+        load_x(1)
+        load_x(2)
+        load_w(w3[SHARED], w3_words[SHARED])
+        load_scales(w3s, w3_scales.rearrange("e s q c -> (e s) q c"))
+        load_w(w1[0], w1_words[0])
+        load_scales(w1s_routed, w1_scales[0:E].rearrange("e s q c -> (e s) q c"))
+        load_w(w3[0], w3_words[0])
+        load_w(w1[1], w1_words[1])
+        load_w(w3[1], w3_words[1])
+        load_w(w2, w2_words.rearrange("e s p c -> (e s) p c"))
+        load_scales(w2s, w2_scales.rearrange("e s q c -> (e s) q c"))
+        nc.sync.dma_start(out=gate_sb[:], in_=gate[0:P, :])
+
+        for b in range(BLOCKS):
+            nc.gpsimd.memset(routed[b][:], 0.0)
+
+        def slots(e):
+            return offsets[:, e * C // 16:(e + 1) * C // 16]
+
+        def gather(e):
+            words, scales = [], []
+            for s in range(PASSES):
+                gw = keep.tile([P, C], U32, name="gw%d_%d" % (e, s), align_bytes=64)
+                gs = keep.tile([P, C], U8, name="gs%d_%d" % (e, s), align_bytes=64)
+                nc.vector.tensor_copy(out=gw[:], in_=xw[s][:].indirect(slots(e)))
+                nc.vector.tensor_copy(out=gs[:], in_=xs[:, s, :].indirect(slots(e)))
+                words.append(gw[:])
+                scales.append(gs[:])
+            return words, scales
+
+        def product(bank, e, m, operands, j, passes=range(PASSES)):
+            words, scales = operands
+            cols = slice(j * P, (j + 1) * P)
+            for s in passes:
+                if m == 1:
+                    plane = w3s[:, e * PASSES + s, :]
+                elif e == SHARED:
+                    plane = w1s_shared[:, s, :]
+                else:
+                    plane = w1s_routed[:, e * PASSES + s, :]
+                nc.tensor.matmul_mx(
+                    out=bank[:],
+                    lhsT=words[s][:, cols].bitcast(FP8X4),
+                    lhsT_scale=scales[s][:, cols],
+                    rhs=(w1, w3)[m][e][:, s, :].bitcast(FP4X4),
+                    rhs_scale=plane,
+                    start=(s == 0),
+                    stop=(s == PASSES - 1),
+                )
+
+        def gated(a1, a3):
+            act = work.tile([P, H], F32, name="act", tag="act", bufs=4)
+            h = work.tile([P, H], BF16, name="h", tag="h", bufs=12, align_bytes=64)
+            nc.scalar.activation(
+                out=act[:].rearrange("t (u p v) -> t u p v", u=2, v=2),
+                in_=a1[:].rearrange("t (p u v) -> t u p v", u=2, v=2),
+                func=SILU,
+            )
+            nc.vector.tensor_tensor(
+                out=h[:].rearrange("t (u p v) -> t u p v", u=2, v=2),
+                in0=a3[:].rearrange("t (p u v) -> t u p v", u=2, v=2),
+                in1=act[:].rearrange("t (u p v) -> t u p v", u=2, v=2),
+                op=MULT,
+            )
+            return h
+
+        def first_layer(place, e, operands, j):
+            a1, a3 = banks[place % 2], banks[2 + place % 3]
+            product(a1, e, 0, operands, j)
+            product(a3, e, 1, operands, j)
+            return gated(a1, a3)
+
+        def turn(hidden, bank, grouped):
+            n = len(hidden)
+            turned = bank[:, 0:n * 2 * P].rearrange("p (j u t) -> p j u t", j=n, u=2)
+            for j, h in enumerate(hidden):
+                for u in range(2):
+                    nc.tensor.transpose(turned[:, j, u, :], h[:].bitcast(F32)[:, u * P:(u + 1) * P], ident[:])
+            nc.scalar.copy(
+                out=grouped.bitcast(F32).rearrange("p (j t u) -> p j t u", j=n, u=2),
+                in_=turned.rearrange("p j u t -> p j t u"),
+            )
+
+        def quantise(grouped, name):
+            width = grouped.shape[1] // 4
+            hw = keep.tile([P, width], U32, name="hw" + name, align_bytes=64)
+            hs = keep.tile([P, width], U8, name="hs" + name, align_bytes=64)
+            nc.vector.quantize_mx(out=hw[:].bitcast(FP8X4), scales=hs[:], in_=grouped[:])
+            return hw[:], hs[:]
+
+        def staged(name, width):
+            return keep.tile([P, 4 * width], BF16, name="grouped" + name, align_bytes=64)
+
+        def second_layer(y, e, b, hw, hs):
+            nc.tensor.matmul_mx(
+                out=y,
+                lhsT=w2[:, e, 2 * b * P:2 * (b + 1) * P].bitcast(FP4X4),
+                lhsT_scale=w2s[:, e, b * P:(b + 1) * P],
+                rhs=hw.bitcast(FP8X4),
+                rhs_scale=hs,
+                start=True,
+                stop=True,
+            )
+
+        def scatter(e, b, hw, hs):
+            y = banks[6 + (e * BLOCKS + b) % 2][:, 0:C]
+            second_layer(y, e, b, hw, hs)
+            y_sb = work.tile([P, C], F32, name="y_sb", tag="y_sb", bufs=E * BLOCKS)
+            nc.scalar.copy(out=y_sb[:], in_=y)
+            nc.vector.tensor_tensor(
+                out=routed[b][:].indirect(slots(e)), in0=y_sb[:], in1=gate_sb[:, e * C:(e + 1) * C], op=MULT
+            )
+
+        def finish(cols, hw, hs, bank_ids):
+            width = cols.stop - cols.start
+            for b in range(BLOCKS):
+                y = banks[bank_ids[b]][:, 0:width]
+                second_layer(y, SHARED, b, hw, hs)
+                result = work.tile([P, width], F32, name="result", tag="result", bufs=12)
+                nc.vector.tensor_tensor(out=result[:], in0=y, in1=routed[b][:, cols], op=ADD)
+                nc.sync.dma_start(out=out[b * P:(b + 1) * P, cols], in_=result[:])
+
+        def tokens(g):
+            cols = slice(g * GROUP, (g + 1) * GROUP)
+            return [xw[s][:, cols] for s in range(PASSES)], [xs[:, s, cols] for s in range(PASSES)]
+
+        gathered = [gather(e) for e in range(E)]
+
+        for s in range(PASSES):
+            for j in range(2):
+                product(banks[j], SHARED, 0, tokens(0), j, [s])
+        hs = []
+        for j in range(2):
+            product(banks[2 + j], SHARED, 1, tokens(0), j)
+            hs.append(gated(banks[j], banks[2 + j]))
+        hr = [first_layer(2, 0, gathered[0], 0), first_layer(3, 0, gathered[0], 1)]
+        hr.append(first_layer(4, 1, gathered[1], 0))
+        g_r0 = staged("r0", C)
+        turn(hr[0:2], banks[5], g_r0[:])
+        q_r0 = quantise(g_r0, "r0")
+        hr.append(first_layer(5, 1, gathered[1], 1))
+        scatter(0, 0, *q_r0)
+        hs.append(first_layer(6, SHARED, tokens(1), 0))
+        g_r1 = staged("r1", C)
+        turn(hr[2:4], banks[5], g_r1[:])
+        q_r1 = quantise(g_r1, "r1")
+        scatter(0, 1, *q_r0)
+        hs.append(first_layer(7, SHARED, tokens(1), 1))
+        scatter(0, 2, *q_r0)
+        g_s01 = staged("s01", 2 * GROUP)
+        turn(hs[0:2], banks[5], g_s01[:, 0:4 * GROUP])
+        hs.append(first_layer(8, SHARED, tokens(2), 0))
+        scatter(1, 0, *q_r1)
+        hs.append(first_layer(9, SHARED, tokens(2), 1))
+        scatter(1, 1, *q_r1)
+        turn(hs[2:4], banks[5], g_s01[:, 4 * GROUP:8 * GROUP])
+        q_s01 = quantise(g_s01, "s01")
+        hs.append(first_layer(10, SHARED, tokens(3), 0))
+        scatter(1, 2, *q_r1)
+        hs.append(first_layer(11, SHARED, tokens(3), 1))
+        g_s23 = staged("s23", 2 * GROUP)
+        turn(hs[4:6], banks[5], g_s23[:, 0:4 * GROUP])
+        finish(slice(0, 2 * GROUP), *q_s01, (6, 0, 2))
+        turn(hs[6:8], banks[1], g_s23[:, 4 * GROUP:8 * GROUP])
+        q_s23 = quantise(g_s23, "s23")
+        finish(slice(2 * GROUP, 4 * GROUP), *q_s23, (7, 3, 4))

@@ -40,9 +40,10 @@ def tile_moe_shr_glu_silu_kernel(
         w1 = [keep.tile([P, PASSES, 2 * H], U8, name="w1_%d" % e, align_bytes=64) for e in range(E + 1)]
         w3 = [keep.tile([P, PASSES, 2 * H], U8, name="w3_%d" % e, align_bytes=64) for e in range(E + 1)]
         w2 = keep.tile([P, E + 1, 2 * N], U8, name="w2", align_bytes=64)
-        w1s_shared = keep.tile([P, PASSES, H], U8, name="w1s_shared", align_bytes=64)
-        w1s_routed = keep.tile([P, E * PASSES, H], U8, name="w1s_routed", align_bytes=64)
-        w3s = keep.tile([P, (E + 1) * PASSES, H], U8, name="w3s", align_bytes=64)
+        w1s_first = keep.tile([P, PASSES, H], U8, name="w1s_first", align_bytes=64)
+        w1s_rest = keep.tile([P, E * PASSES, H], U8, name="w1s_rest", align_bytes=64)
+        w3s_first = keep.tile([P, PASSES, H], U8, name="w3s_first", align_bytes=64)
+        w3s_rest = keep.tile([P, E * PASSES, H], U8, name="w3s_rest", align_bytes=64)
         w2s = keep.tile([P, E + 1, N], U8, name="w2s", align_bytes=64)
         gate_sb = keep.tile([P, E * C], F32, name="gate_sb")
         routed = [keep.tile([P, T], F32, name="routed%d" % b) for b in range(BLOCKS)]
@@ -60,29 +61,30 @@ def tile_moe_shr_glu_silu_kernel(
         def load_w(tile, words):
             nc.sync.dma_start(out=tile[:].bitcast(I32), in_=words.rearrange("s p c -> p s c").bitcast(I32))
 
-        nc.gpsimd.memset(w1s_shared[:].bitcast(I32), 0)
-        for plane in (xs, w3s, w1s_routed, w2s):
+        nc.gpsimd.memset(xs[:, 0:2, :].bitcast(I32), 0)
+        nc.vector.memset(xs[:, 2:3, :].bitcast(I32), 0)
+        for plane in (w1s_first, w3s_first, w1s_rest, w3s_rest, w2s):
             nc.vector.memset(plane[:].bitcast(I32), 0)
         make_identity(nc, ident[:])
         nc.scalar.activation(out=warm[:, 0:1], in_=ident[:, 0:1], func=SILU)
 
-        load_x(0)
-        load_w(w1[SHARED], w1_words[SHARED])
         nc.sync.dma_start(offsets[:], offs)
-        load_scales(w1s_shared, w1_scales[SHARED])
+        for s in range(PASSES):
+            load_x(s)
         load_scales(xs, x_scales)
-        load_x(1)
-        load_x(2)
-        load_w(w3[SHARED], w3_words[SHARED])
-        load_scales(w3s, w3_scales.rearrange("e s q c -> (e s) q c"))
         load_w(w1[0], w1_words[0])
-        load_scales(w1s_routed, w1_scales[0:E].rearrange("e s q c -> (e s) q c"))
+        load_scales(w1s_first, w1_scales[0])
         load_w(w3[0], w3_words[0])
-        load_w(w1[1], w1_words[1])
-        load_w(w3[1], w3_words[1])
+        load_scales(w3s_first, w3_scales[0])
         load_w(w2, w2_words.rearrange("e s p c -> (e s) p c"))
         load_scales(w2s, w2_scales.rearrange("e s q c -> (e s) q c"))
         nc.sync.dma_start(out=gate_sb[:], in_=gate[0:P, :])
+        load_w(w1[1], w1_words[1])
+        load_scales(w1s_rest, w1_scales[1:E + 1].rearrange("e s q c -> (e s) q c"))
+        load_w(w3[1], w3_words[1])
+        load_scales(w3s_rest, w3_scales[1:E + 1].rearrange("e s q c -> (e s) q c"))
+        load_w(w1[SHARED], w1_words[SHARED])
+        load_w(w3[SHARED], w3_words[SHARED])
 
         for b in range(BLOCKS):
             nc.gpsimd.memset(routed[b][:], 0.0)
@@ -90,14 +92,18 @@ def tile_moe_shr_glu_silu_kernel(
         def slots(e):
             return offsets[:, e * C // 16:(e + 1) * C // 16]
 
+        slot_words = []
+        for s in range(PASSES):
+            gw = keep.tile([P, E * C], U32, name="gw%d" % s, align_bytes=64)
+            nc.vector.tensor_copy(out=gw[:], in_=xw[s][:].indirect(offsets[:]))
+            slot_words.append(gw)
+
         def gather(e):
             words, scales = [], []
             for s in range(PASSES):
-                gw = keep.tile([P, C], U32, name="gw%d_%d" % (e, s), align_bytes=64)
                 gs = keep.tile([P, C], U8, name="gs%d_%d" % (e, s), align_bytes=64)
-                nc.vector.tensor_copy(out=gw[:], in_=xw[s][:].indirect(slots(e)))
                 nc.vector.tensor_copy(out=gs[:], in_=xs[:, s, :].indirect(slots(e)))
-                words.append(gw[:])
+                words.append(slot_words[s][:, e * C:(e + 1) * C])
                 scales.append(gs[:])
             return words, scales
 
@@ -105,12 +111,10 @@ def tile_moe_shr_glu_silu_kernel(
             words, scales = operands
             cols = slice(j * P, (j + 1) * P)
             for s in passes:
-                if m == 1:
-                    plane = w3s[:, e * PASSES + s, :]
-                elif e == SHARED:
-                    plane = w1s_shared[:, s, :]
+                if e == 0:
+                    plane = (w1s_first, w3s_first)[m][:, s, :]
                 else:
-                    plane = w1s_routed[:, e * PASSES + s, :]
+                    plane = (w1s_rest, w3s_rest)[m][:, (e - 1) * PASSES + s, :]
                 nc.tensor.matmul_mx(
                     out=bank[:],
                     lhsT=words[s][:, cols].bitcast(FP8X4),
@@ -121,14 +125,17 @@ def tile_moe_shr_glu_silu_kernel(
                     stop=(s == PASSES - 1),
                 )
 
-        def gated(a1, a3):
-            act = work.tile([P, H], F32, name="act", tag="act", bufs=4)
-            h = work.tile([P, H], BF16, name="h", tag="h", bufs=12, align_bytes=64)
+        def silu(a1):
+            act = work.tile([P, H], F32, name="act", tag="act", bufs=12)
             nc.scalar.activation(
                 out=act[:].rearrange("t (u p v) -> t u p v", u=2, v=2),
                 in_=a1[:].rearrange("t (p u v) -> t u p v", u=2, v=2),
                 func=SILU,
             )
+            return act
+
+        def gated(act, a3):
+            h = work.tile([P, H], BF16, name="h", tag="h", bufs=12, align_bytes=64)
             nc.vector.tensor_tensor(
                 out=h[:].rearrange("t (u p v) -> t u p v", u=2, v=2),
                 in0=a3[:].rearrange("t (p u v) -> t u p v", u=2, v=2),
@@ -136,12 +143,6 @@ def tile_moe_shr_glu_silu_kernel(
                 op=MULT,
             )
             return h
-
-        def first_layer(place, e, operands, j):
-            a1, a3 = banks[place % 2], banks[2 + place % 3]
-            product(a1, e, 0, operands, j)
-            product(a3, e, 1, operands, j)
-            return gated(a1, a3)
 
         def turn(hidden, bank, grouped):
             n = len(hidden)
@@ -175,8 +176,8 @@ def tile_moe_shr_glu_silu_kernel(
                 stop=True,
             )
 
-        def scatter(e, b, hw, hs):
-            y = banks[6 + (e * BLOCKS + b) % 2][:, 0:C]
+        def scatter(bank, e, b, hw, hs):
+            y = bank[:, 0:C]
             second_layer(y, e, b, hw, hs)
             y_sb = work.tile([P, C], F32, name="y_sb", tag="y_sb", bufs=E * BLOCKS)
             nc.scalar.copy(out=y_sb[:], in_=y)
@@ -193,47 +194,81 @@ def tile_moe_shr_glu_silu_kernel(
                 nc.vector.tensor_tensor(out=result[:], in0=y, in1=routed[b][:, cols], op=ADD)
                 nc.sync.dma_start(out=out[b * P:(b + 1) * P, cols], in_=result[:])
 
+        def finish_aside(cols, hw, hs, bank_ids):
+            width = cols.stop - cols.start
+            for b in range(BLOCKS):
+                y = banks[bank_ids[b]][:, 0:width]
+                second_layer(y, SHARED, b, hw, hs)
+                ys = work.tile([P, width], F32, name="ys", tag="ys", bufs=BLOCKS)
+                nc.scalar.copy(out=ys[:], in_=y)
+                result = work.tile([P, width], F32, name="result", tag="result", bufs=12)
+                nc.gpsimd.tensor_tensor(out=result[:], in0=ys[:], in1=routed[b][:, cols], op=ADD)
+                nc.sync.dma_start(out=out[b * P:(b + 1) * P, cols], in_=result[:])
+
         def tokens(g):
             cols = slice(g * GROUP, (g + 1) * GROUP)
             return [xw[s][:, cols] for s in range(PASSES)], [xs[:, s, cols] for s in range(PASSES)]
 
+        up_banks = (2, 3, 4, 6)
+        acts = {}
+
+        def left(place, e, operands, j):
+            product(banks[place % 2], e, 0, operands, j)
+            acts[place] = silu(banks[place % 2])
+
+        def right(place, e, operands, j):
+            bank = banks[up_banks[place % len(up_banks)]]
+            product(bank, e, 1, operands, j)
+            return gated(acts[place], bank)
+
+        def both(place, e, operands, j):
+            left(place, e, operands, j)
+            return right(place, e, operands, j)
+
         gathered = [gather(e) for e in range(E)]
+        g_r0 = staged("r0", C)
+        g_r1 = staged("r1", C)
+        g_s01 = staged("s01", 2 * GROUP)
+        g_s2 = staged("s2", GROUP)
+        g_s3 = staged("s3", GROUP)
 
         for s in range(PASSES):
             for j in range(2):
-                product(banks[j], SHARED, 0, tokens(0), j, [s])
-        hs = []
+                product(banks[j], 0, 0, gathered[0], j, [s])
         for j in range(2):
-            product(banks[2 + j], SHARED, 1, tokens(0), j)
-            hs.append(gated(banks[j], banks[2 + j]))
-        hr = [first_layer(2, 0, gathered[0], 0), first_layer(3, 0, gathered[0], 1)]
-        hr.append(first_layer(4, 1, gathered[1], 0))
-        g_r0 = staged("r0", C)
+            acts[j] = silu(banks[j])
+        hr = [right(j, 0, gathered[0], j) for j in range(2)]
         turn(hr[0:2], banks[5], g_r0[:])
         q_r0 = quantise(g_r0, "r0")
-        hr.append(first_layer(5, 1, gathered[1], 1))
-        scatter(0, 0, *q_r0)
-        hs.append(first_layer(6, SHARED, tokens(1), 0))
-        g_r1 = staged("r1", C)
-        turn(hr[2:4], banks[5], g_r1[:])
+        left(2, 1, gathered[1], 0)
+        left(3, 1, gathered[1], 1)
+        scatter(banks[0], 0, 0, *q_r0)
+        hr.append(right(2, 1, gathered[1], 0))
+        hr.append(right(3, 1, gathered[1], 1))
+        left(4, SHARED, tokens(0), 0)
+        left(5, SHARED, tokens(0), 1)
+        scatter(banks[0], 0, 1, *q_r0)
+        hs = [right(4, SHARED, tokens(0), 0)]
+        turn(hr[2:4], banks[1], g_r1[:])
         q_r1 = quantise(g_r1, "r1")
-        scatter(0, 1, *q_r0)
-        hs.append(first_layer(7, SHARED, tokens(1), 1))
-        scatter(0, 2, *q_r0)
-        g_s01 = staged("s01", 2 * GROUP)
+        hs.append(right(5, SHARED, tokens(0), 1))
+        hs.append(both(6, SHARED, tokens(1), 0))
+        scatter(banks[0], 0, 2, *q_r0)
+        hs.append(both(7, SHARED, tokens(1), 1))
+        scatter(banks[1], 1, 0, *q_r1)
+        hs.append(both(8, SHARED, tokens(2), 0))
+        scatter(banks[0], 1, 1, *q_r1)
         turn(hs[0:2], banks[5], g_s01[:, 0:4 * GROUP])
-        hs.append(first_layer(8, SHARED, tokens(2), 0))
-        scatter(1, 0, *q_r1)
-        hs.append(first_layer(9, SHARED, tokens(2), 1))
-        scatter(1, 1, *q_r1)
+        hs.append(both(9, SHARED, tokens(2), 1))
+        scatter(banks[1], 1, 2, *q_r1)
         turn(hs[2:4], banks[5], g_s01[:, 4 * GROUP:8 * GROUP])
         q_s01 = quantise(g_s01, "s01")
-        hs.append(first_layer(10, SHARED, tokens(3), 0))
-        scatter(1, 2, *q_r1)
-        hs.append(first_layer(11, SHARED, tokens(3), 1))
-        g_s23 = staged("s23", 2 * GROUP)
-        turn(hs[4:6], banks[5], g_s23[:, 0:4 * GROUP])
-        finish(slice(0, 2 * GROUP), *q_s01, (6, 0, 2))
-        turn(hs[6:8], banks[1], g_s23[:, 4 * GROUP:8 * GROUP])
-        q_s23 = quantise(g_s23, "s23")
-        finish(slice(2 * GROUP, 4 * GROUP), *q_s23, (7, 3, 4))
+        hs.append(both(10, SHARED, tokens(3), 0))
+        hs.append(both(11, SHARED, tokens(3), 1))
+        finish(slice(0, 2 * GROUP), *q_s01, (0, 7, 2))
+        turn(hs[4:6], banks[5], g_s2[:])
+        q_s2 = quantise(g_s2, "s2")
+        turn(hs[6:8], banks[1], g_s3[:])
+        q_s3 = quantise(g_s3, "s3")
+        finish(slice(2 * GROUP, 3 * GROUP), *q_s2, (3, 4, 5))
+        finish(slice(3 * GROUP, 4 * GROUP), *q_s3, (6, 1, 0))

@@ -19,10 +19,19 @@ ADD = mybir.AluOpType.add
 SILU = mybir.ActivationFunctionType.Silu
 
 P = 128
-PASSES = K // 512
+PACK = 4
+PASSES = K // (P * PACK)
 SHARED = E
 BLOCKS = N // P
-GROUP = 256
+PER_COLUMN = 16
+PAIR = 2 * P
+ROUTED_TILES = E * C // P
+TILES = ROUTED_TILES + T // P
+W1, W3 = 0, 1
+W1_BANKS = (0, 1)
+W3_BANKS = (2, 3, 4, 6)
+SPARE_BANKS = (5, 7)
+WARM_UPS = 3
 
 
 def tile_moe_shr_glu_silu_kernel(
@@ -34,26 +43,30 @@ def tile_moe_shr_glu_silu_kernel(
         work = ctx.enter_context(tc.tile_pool(name="work", bufs=1))
         psum = ctx.enter_context(tc.psum_pool(name="psum", bufs=1))
 
-        offsets = keep.tile([P, E * C // 16], U16, name="offsets")
+        offsets = keep.tile([P, E * C // PER_COLUMN], U16, name="offsets")
         xw = [keep.tile([P, T], U32, name="xw%d" % s, align_bytes=64) for s in range(PASSES)]
         xs = keep.tile([P, PASSES, T], U8, name="xs", align_bytes=64)
-        w1 = [keep.tile([P, PASSES, 2 * H], U8, name="w1_%d" % e, align_bytes=64) for e in range(E + 1)]
-        w3 = [keep.tile([P, PASSES, 2 * H], U8, name="w3_%d" % e, align_bytes=64) for e in range(E + 1)]
+        w1_head = keep.tile([P, 1, 2 * H], U8, name="w1_head", align_bytes=64)
+        w1 = [
+            keep.tile([P, PASSES - (e == 0), 2 * H], U8, name="w1_%d" % e, tag="w1_%d" % e, align_bytes=64)
+            for e in range(E + 1)
+        ]
+        w3 = [keep.tile([P, PASSES, 2 * H], U8, name="w3_%d" % e, tag="w3_%d" % e, align_bytes=64) for e in range(E + 1)]
         w2 = keep.tile([P, E + 1, 2 * N], U8, name="w2", align_bytes=64)
-        w1s_first = keep.tile([P, PASSES, H], U8, name="w1s_first", align_bytes=64)
+        w1s_first = keep.tile([P, PASSES, H], U8, name="w1s_first", tag="w1s_first", align_bytes=64)
         w1s_rest = keep.tile([P, E * PASSES, H], U8, name="w1s_rest", align_bytes=64)
         w3s_first = keep.tile([P, PASSES, H], U8, name="w3s_first", align_bytes=64)
         w3s_rest = keep.tile([P, E * PASSES, H], U8, name="w3s_rest", align_bytes=64)
         w2s = keep.tile([P, E + 1, N], U8, name="w2s", align_bytes=64)
         gate_sb = keep.tile([P, E * C], F32, name="gate_sb")
-        routed = [keep.tile([P, T], F32, name="routed%d" % b) for b in range(BLOCKS)]
         ident = keep.tile([P, P], F32, name="ident")
-        warm = keep.tile([P, 8], F32, name="warm")
-        banks = [psum.tile([P, 512], F32, name="bank%d" % i) for i in range(8)]
+        banks = [psum.tile([P, H], F32, name="bank%d" % i) for i in range(8)]
 
-        def load_scales(plane, rows):
-            for r in range(4):
-                nc.sync.dma_start(out=plane[r:P:32].bitcast(I32), in_=rows[:, r:16:4, :].rearrange("s q c -> q s c").bitcast(I32))
+        def load_scales(plane, rows, quarters=range(4)):
+            for r in quarters:
+                nc.sync.dma_start(
+                    out=plane[r:P:32].bitcast(I32), in_=rows[:, r:16:4, :].rearrange("s q c -> q s c").bitcast(I32)
+                )
 
         def load_x(s):
             nc.sync.dma_start(out=xw[s][:].bitcast(I32), in_=x_words[s].rearrange("p t r -> p (t r)").bitcast(I32))
@@ -61,214 +74,218 @@ def tile_moe_shr_glu_silu_kernel(
         def load_w(tile, words):
             nc.sync.dma_start(out=tile[:].bitcast(I32), in_=words.rearrange("s p c -> p s c").bitcast(I32))
 
-        nc.gpsimd.memset(xs[:, 0:2, :].bitcast(I32), 0)
-        nc.vector.memset(xs[:, 2:3, :].bitcast(I32), 0)
-        for plane in (w1s_first, w3s_first, w1s_rest, w3s_rest, w2s):
+        def by_pass(packed):
+            return packed.rearrange("e s p c -> (e s) p c")
+
+        nc.gpsimd.memset(w1s_first[:].bitcast(I32), 0)
+        for plane in (xs, w3s_first, w1s_rest, w3s_rest, w2s):
             nc.vector.memset(plane[:].bitcast(I32), 0)
         make_identity(nc, ident[:])
-        nc.scalar.activation(out=warm[:, 0:1], in_=ident[:, 0:1], func=SILU)
 
         nc.sync.dma_start(offsets[:], offs)
-        for s in range(PASSES):
-            load_x(s)
-        load_scales(xs, x_scales)
-        load_w(w1[0], w1_words[0])
+        load_x(0)
+        load_x(1)
         load_scales(w1s_first, w1_scales[0])
+        load_x(2)
+        load_w(w1_head, w1_words[0, 0:1])
+        load_scales(xs, x_scales)
+        load_w(w1[0], w1_words[0, 1:PASSES])
         load_w(w3[0], w3_words[0])
         load_scales(w3s_first, w3_scales[0])
-        load_w(w2, w2_words.rearrange("e s p c -> (e s) p c"))
-        load_scales(w2s, w2_scales.rearrange("e s q c -> (e s) q c"))
-        nc.sync.dma_start(out=gate_sb[:], in_=gate[0:P, :])
+        load_w(w2, by_pass(w2_words))
+        load_scales(w2s, by_pass(w2_scales), range(3))
         load_w(w1[1], w1_words[1])
-        load_scales(w1s_rest, w1_scales[1:E + 1].rearrange("e s q c -> (e s) q c"))
+        load_scales(w1s_rest, by_pass(w1_scales[1:E + 1]))
+        load_scales(w2s, by_pass(w2_scales), [3])
+        nc.sync.dma_start(out=gate_sb[:], in_=gate[0:P, :])
         load_w(w3[1], w3_words[1])
-        load_scales(w3s_rest, w3_scales[1:E + 1].rearrange("e s q c -> (e s) q c"))
+        load_scales(w3s_rest, by_pass(w3_scales[1:E + 1]))
         load_w(w1[SHARED], w1_words[SHARED])
         load_w(w3[SHARED], w3_words[SHARED])
 
-        for b in range(BLOCKS):
-            nc.gpsimd.memset(routed[b][:], 0.0)
-
         def slots(e):
-            return offsets[:, e * C // 16:(e + 1) * C // 16]
+            return offsets[:, e * C // PER_COLUMN:(e + 1) * C // PER_COLUMN]
 
         slot_words = []
         for s in range(PASSES):
             gw = keep.tile([P, E * C], U32, name="gw%d" % s, align_bytes=64)
             nc.vector.tensor_copy(out=gw[:], in_=xw[s][:].indirect(offsets[:]))
             slot_words.append(gw)
-
-        def gather(e):
-            words, scales = [], []
+        slot_scales = {}
+        for e in range(E):
             for s in range(PASSES):
-                gs = keep.tile([P, C], U8, name="gs%d_%d" % (e, s), align_bytes=64)
-                nc.vector.tensor_copy(out=gs[:], in_=xs[:, s, :].indirect(slots(e)))
-                words.append(slot_words[s][:, e * C:(e + 1) * C])
-                scales.append(gs[:])
-            return words, scales
+                slot_scales[e, s] = keep.tile([P, C], U8, name="gs%d_%d" % (e, s), align_bytes=64)
+                nc.vector.tensor_copy(out=slot_scales[e, s][:], in_=xs[:, s, :].indirect(slots(e)))
 
-        def product(bank, e, m, operands, j, passes=range(PASSES)):
-            words, scales = operands
-            cols = slice(j * P, (j + 1) * P)
-            for s in passes:
-                if e == 0:
-                    plane = (w1s_first, w3s_first)[m][:, s, :]
-                else:
-                    plane = (w1s_rest, w3s_rest)[m][:, (e - 1) * PASSES + s, :]
-                nc.tensor.matmul_mx(
-                    out=bank[:],
-                    lhsT=words[s][:, cols].bitcast(FP8X4),
-                    lhsT_scale=scales[s][:, cols],
-                    rhs=(w1, w3)[m][e][:, s, :].bitcast(FP4X4),
-                    rhs_scale=plane,
-                    start=(s == 0),
-                    stop=(s == PASSES - 1),
-                )
+        def stationary(tile, s):
+            if tile < ROUTED_TILES:
+                e, place = divmod(tile * P, C)
+                return e, slot_words[s][:, tile * P:(tile + 1) * P], slot_scales[e, s][:, place:place + P]
+            cols = slice((tile - ROUTED_TILES) * P, (tile - ROUTED_TILES + 1) * P)
+            return SHARED, xw[s][:, cols], xs[:, s, cols]
 
-        def silu(a1):
-            act = work.tile([P, H], F32, name="act", tag="act", bufs=12)
+        def moving(matrix, e, s):
+            if e > 0:
+                return (w1, w3)[matrix][e][:, s, :], (w1s_rest, w3s_rest)[matrix][:, (e - 1) * PASSES + s, :]
+            if matrix == W3:
+                return w3[0][:, s, :], w3s_first[:, s, :]
+            return (w1_head[:, 0, :] if s == 0 else w1[0][:, s - 1, :]), w1s_first[:, s, :]
+
+        def w1_bank(tile):
+            return banks[W1_BANKS[tile % len(W1_BANKS)]]
+
+        def w3_bank(tile):
+            return banks[W3_BANKS[tile % len(W3_BANKS)]]
+
+        def first_layer_pass(bank, tile, matrix, s):
+            e, words, scales = stationary(tile, s)
+            weights, plane = moving(matrix, e, s)
+            nc.tensor.matmul_mx(
+                out=bank[:],
+                lhsT=words.bitcast(FP8X4),
+                lhsT_scale=scales,
+                rhs=weights.bitcast(FP4X4),
+                rhs_scale=plane,
+                start=(s == 0),
+                stop=(s == PASSES - 1),
+            )
+
+        acts = {}
+        hidden = {}
+
+        def silu(tile):
+            acts[tile] = work.tile([P, H], F32, name="act", tag="act", bufs=TILES)
             nc.scalar.activation(
-                out=act[:].rearrange("t (u p v) -> t u p v", u=2, v=2),
-                in_=a1[:].rearrange("t (p u v) -> t u p v", u=2, v=2),
+                out=acts[tile][:].rearrange("t (u p v) -> t u p v", u=2, v=2),
+                in_=w1_bank(tile)[:].rearrange("t (p u v) -> t u p v", u=2, v=2),
                 func=SILU,
             )
-            return act
 
-        def gated(act, a3):
-            h = work.tile([P, H], BF16, name="h", tag="h", bufs=12, align_bytes=64)
+        def w1_side(tile):
+            for s in range(PASSES):
+                first_layer_pass(w1_bank(tile), tile, W1, s)
+            silu(tile)
+
+        def w3_side(tile):
+            for s in range(PASSES):
+                first_layer_pass(w3_bank(tile), tile, W3, s)
+            hidden[tile] = work.tile([P, H], BF16, name="h", tag="h", bufs=TILES, align_bytes=64)
             nc.vector.tensor_tensor(
-                out=h[:].rearrange("t (u p v) -> t u p v", u=2, v=2),
-                in0=a3[:].rearrange("t (p u v) -> t u p v", u=2, v=2),
-                in1=act[:].rearrange("t (u p v) -> t u p v", u=2, v=2),
+                out=hidden[tile][:].rearrange("t (u p v) -> t u p v", u=2, v=2),
+                in0=w3_bank(tile)[:].rearrange("t (p u v) -> t u p v", u=2, v=2),
+                in1=acts[tile][:].rearrange("t (u p v) -> t u p v", u=2, v=2),
                 op=MULT,
             )
-            return h
 
-        def turn(hidden, bank, grouped):
-            n = len(hidden)
-            turned = bank[:, 0:n * 2 * P].rearrange("p (j u t) -> p j u t", j=n, u=2)
-            for j, h in enumerate(hidden):
-                for u in range(2):
-                    nc.tensor.transpose(turned[:, j, u, :], h[:].bitcast(F32)[:, u * P:(u + 1) * P], ident[:])
-            nc.scalar.copy(
-                out=grouped.bitcast(F32).rearrange("p (j t u) -> p j t u", j=n, u=2),
-                in_=turned.rearrange("p j u t -> p j t u"),
-            )
+        def first_layer(tile):
+            w1_side(tile)
+            w3_side(tile)
 
-        def quantise(grouped, name):
-            width = grouped.shape[1] // 4
-            hw = keep.tile([P, width], U32, name="hw" + name, align_bytes=64)
-            hs = keep.tile([P, width], U8, name="hs" + name, align_bytes=64)
+        def quantised(first_tile, pair_banks):
+            width = len(pair_banks) * PAIR
+            grouped = keep.tile([P, PACK * width], BF16, name="grouped%d" % first_tile, align_bytes=64)
+            for n, bank in enumerate(pair_banks):
+                turned = bank[:].rearrange("p (j u t) -> p j u t", j=2, u=2)
+                for j in range(2):
+                    pairs = hidden[first_tile + 2 * n + j][:].bitcast(F32)
+                    for u in range(2):
+                        nc.tensor.transpose(turned[:, j, u, :], pairs[:, u * P:(u + 1) * P], ident[:])
+                nc.scalar.copy(
+                    out=grouped[:, n * PACK * PAIR:(n + 1) * PACK * PAIR].bitcast(F32).rearrange("p (j t u) -> p j t u", j=2, u=2),
+                    in_=turned.rearrange("p j u t -> p j t u"),
+                )
+            hw = keep.tile([P, width], U32, name="hw%d" % first_tile, align_bytes=64)
+            hs = keep.tile([P, width], U8, name="hs%d" % first_tile, align_bytes=64)
             nc.vector.quantize_mx(out=hw[:].bitcast(FP8X4), scales=hs[:], in_=grouped[:])
-            return hw[:], hs[:]
+            return hw, hs
 
-        def staged(name, width):
-            return keep.tile([P, 4 * width], BF16, name="grouped" + name, align_bytes=64)
-
-        def second_layer(y, e, b, hw, hs):
+        def second_layer(y, e, b, codes):
+            hw, hs = codes
             nc.tensor.matmul_mx(
                 out=y,
                 lhsT=w2[:, e, 2 * b * P:2 * (b + 1) * P].bitcast(FP4X4),
                 lhsT_scale=w2s[:, e, b * P:(b + 1) * P],
-                rhs=hw.bitcast(FP8X4),
-                rhs_scale=hs,
+                rhs=hw[:].bitcast(FP8X4),
+                rhs_scale=hs[:],
                 start=True,
                 stop=True,
             )
 
-        def scatter(bank, e, b, hw, hs):
-            y = bank[:, 0:C]
-            second_layer(y, e, b, hw, hs)
-            y_sb = work.tile([P, C], F32, name="y_sb", tag="y_sb", bufs=E * BLOCKS)
-            nc.scalar.copy(out=y_sb[:], in_=y)
-            nc.vector.tensor_tensor(
-                out=routed[b][:].indirect(slots(e)), in0=y_sb[:], in1=gate_sb[:, e * C:(e + 1) * C], op=MULT
+        windows = []
+
+        def scatter(e, blocks, codes, bank):
+            for n, b in enumerate(blocks):
+                second_layer(bank[:, n * C:(n + 1) * C], e, b, codes)
+            y_sb = work.tile([P, len(blocks) * C], F32, name="y_sb", tag="y_sb", bufs=E * BLOCKS - 1)
+            nc.scalar.copy(out=y_sb[:], in_=bank[:, 0:len(blocks) * C])
+            for n, b in enumerate(blocks):
+                nc.vector.tensor_tensor(
+                    out=windows[b][:].indirect(slots(e)),
+                    in0=y_sb[:, n * C:(n + 1) * C],
+                    in1=gate_sb[:, e * C:(e + 1) * C],
+                    op=MULT,
+                )
+
+        def finish(first_tile, codes, block_banks):
+            first = (first_tile - ROUTED_TILES) * P
+            width = codes[0].shape[1]
+            for b, bank in enumerate(block_banks):
+                second_layer(bank[:, 0:width], SHARED, b, codes)
+                result = work.tile([P, width], F32, name="result", tag="result", bufs=3 * BLOCKS)
+                nc.vector.tensor_tensor(out=result[:], in0=bank[:, 0:width], in1=windows[b][:, first:first + width], op=ADD)
+                nc.sync.dma_start(out=out[b * P:(b + 1) * P, first:first + width], in_=result[:])
+
+        spare, other_spare = banks[SPARE_BANKS[0]], banks[SPARE_BANKS[1]]
+
+        head_words, head_plane = moving(W1, 0, 0)
+        for warm_up in range(WARM_UPS):
+            nc.tensor.matmul_mx(
+                out=other_spare[:],
+                lhsT=slot_words[0][:, 0:P].bitcast(FP8X4),
+                lhsT_scale=head_plane[:, 0:P],
+                rhs=head_words.bitcast(FP4X4),
+                rhs_scale=head_plane,
+                start=True,
+                stop=True,
             )
 
-        def finish(cols, hw, hs, bank_ids):
-            width = cols.stop - cols.start
-            for b in range(BLOCKS):
-                y = banks[bank_ids[b]][:, 0:width]
-                second_layer(y, SHARED, b, hw, hs)
-                result = work.tile([P, width], F32, name="result", tag="result", bufs=12)
-                nc.vector.tensor_tensor(out=result[:], in0=y, in1=routed[b][:, cols], op=ADD)
-                nc.sync.dma_start(out=out[b * P:(b + 1) * P, cols], in_=result[:])
-
-        def finish_aside(cols, hw, hs, bank_ids):
-            width = cols.stop - cols.start
-            for b in range(BLOCKS):
-                y = banks[bank_ids[b]][:, 0:width]
-                second_layer(y, SHARED, b, hw, hs)
-                ys = work.tile([P, width], F32, name="ys", tag="ys", bufs=BLOCKS)
-                nc.scalar.copy(out=ys[:], in_=y)
-                result = work.tile([P, width], F32, name="result", tag="result", bufs=12)
-                nc.gpsimd.tensor_tensor(out=result[:], in0=ys[:], in1=routed[b][:, cols], op=ADD)
-                nc.sync.dma_start(out=out[b * P:(b + 1) * P, cols], in_=result[:])
-
-        def tokens(g):
-            cols = slice(g * GROUP, (g + 1) * GROUP)
-            return [xw[s][:, cols] for s in range(PASSES)], [xs[:, s, cols] for s in range(PASSES)]
-
-        up_banks = (2, 3, 4, 6)
-        acts = {}
-
-        def left(place, e, operands, j):
-            product(banks[place % 2], e, 0, operands, j)
-            acts[place] = silu(banks[place % 2])
-
-        def right(place, e, operands, j):
-            bank = banks[up_banks[place % len(up_banks)]]
-            product(bank, e, 1, operands, j)
-            return gated(acts[place], bank)
-
-        def both(place, e, operands, j):
-            left(place, e, operands, j)
-            return right(place, e, operands, j)
-
-        gathered = [gather(e) for e in range(E)]
-        g_r0 = staged("r0", C)
-        g_r1 = staged("r1", C)
-        g_s01 = staged("s01", 2 * GROUP)
-        g_s2 = staged("s2", GROUP)
-        g_s3 = staged("s3", GROUP)
-
         for s in range(PASSES):
-            for j in range(2):
-                product(banks[j], 0, 0, gathered[0], j, [s])
-        for j in range(2):
-            acts[j] = silu(banks[j])
-        hr = [right(j, 0, gathered[0], j) for j in range(2)]
-        turn(hr[0:2], banks[5], g_r0[:])
-        q_r0 = quantise(g_r0, "r0")
-        left(2, 1, gathered[1], 0)
-        left(3, 1, gathered[1], 1)
-        scatter(banks[0], 0, 0, *q_r0)
-        hr.append(right(2, 1, gathered[1], 0))
-        hr.append(right(3, 1, gathered[1], 1))
-        left(4, SHARED, tokens(0), 0)
-        left(5, SHARED, tokens(0), 1)
-        scatter(banks[0], 0, 1, *q_r0)
-        hs = [right(4, SHARED, tokens(0), 0)]
-        turn(hr[2:4], banks[1], g_r1[:])
-        q_r1 = quantise(g_r1, "r1")
-        hs.append(right(5, SHARED, tokens(0), 1))
-        hs.append(both(6, SHARED, tokens(1), 0))
-        scatter(banks[0], 0, 2, *q_r0)
-        hs.append(both(7, SHARED, tokens(1), 1))
-        scatter(banks[1], 1, 0, *q_r1)
-        hs.append(both(8, SHARED, tokens(2), 0))
-        scatter(banks[0], 1, 1, *q_r1)
-        turn(hs[0:2], banks[5], g_s01[:, 0:4 * GROUP])
-        hs.append(both(9, SHARED, tokens(2), 1))
-        scatter(banks[1], 1, 2, *q_r1)
-        turn(hs[2:4], banks[5], g_s01[:, 4 * GROUP:8 * GROUP])
-        q_s01 = quantise(g_s01, "s01")
-        hs.append(both(10, SHARED, tokens(3), 0))
-        hs.append(both(11, SHARED, tokens(3), 1))
-        finish(slice(0, 2 * GROUP), *q_s01, (0, 7, 2))
-        turn(hs[4:6], banks[5], g_s2[:])
-        q_s2 = quantise(g_s2, "s2")
-        turn(hs[6:8], banks[1], g_s3[:])
-        q_s3 = quantise(g_s3, "s3")
-        finish(slice(2 * GROUP, 3 * GROUP), *q_s2, (3, 4, 5))
-        finish(slice(3 * GROUP, 4 * GROUP), *q_s3, (6, 1, 0))
+            for tile in (0, 1):
+                first_layer_pass(w1_bank(tile), tile, W1, s)
+        for tile in (0, 1):
+            silu(tile)
+        for tile in (0, 1):
+            w3_side(tile)
+
+        for b, (tag, engine) in enumerate((("w1_0", nc.gpsimd), ("w1s_first", nc.gpsimd), ("w3_0", nc.vector))):
+            windows.append(keep.tile([P, T], F32, name="window%d" % b, tag=tag, align_bytes=64))
+            engine.memset(windows[b][:].bitcast(I32), 0)
+
+        codes_0 = quantised(0, [spare])
+        w1_side(2)
+        scatter(0, [0, 1], codes_0, other_spare)
+        w1_side(3)
+        w3_side(2)
+        w3_side(3)
+
+        w1_side(4)
+        w1_side(5)
+        scatter(0, [2], codes_0, w1_bank(4))
+        w3_side(4)
+        w3_side(5)
+        codes_1 = quantised(2, [w1_bank(5)])
+        first_layer(6)
+        scatter(1, [0], codes_1, w1_bank(6))
+        first_layer(7)
+        scatter(1, [1], codes_1, w1_bank(7))
+        first_layer(8)
+        codes_4_to_7 = quantised(4, [spare, other_spare])
+        scatter(1, [2], codes_1, w1_bank(8))
+        for tile in (9, 10, 11):
+            first_layer(tile)
+
+        finish(4, codes_4_to_7, [other_spare, spare, w1_bank(10)])
+        codes_8_9 = quantised(8, [w3_bank(8)])
+        codes_10_11 = quantised(10, [w1_bank(11)])
+        finish(8, codes_8_9, [w3_bank(9), w3_bank(10), other_spare])
+        finish(10, codes_10_11, [w3_bank(11), spare, w1_bank(10)])

@@ -112,10 +112,14 @@ def tile_moe_shr_glu_silu_kernel(
             nc.vector.tensor_copy(out=gw[:], in_=xw[s][:].indirect(offsets[:]))
             slot_words.append(gw)
         slot_scales = {}
+
+        def gather_scales(e, s, tag):
+            slot_scales[e, s] = keep.tile([P, C], U8, name="gs%d_%d" % (e, s), tag=tag, align_bytes=64)
+            nc.vector.tensor_copy(out=slot_scales[e, s][:], in_=xs[:, s, :].indirect(slots(e)))
+
         for e in range(E):
-            for s in range(PASSES):
-                slot_scales[e, s] = keep.tile([P, C], U8, name="gs%d_%d" % (e, s), align_bytes=64)
-                nc.vector.tensor_copy(out=slot_scales[e, s][:], in_=xs[:, s, :].indirect(slots(e)))
+            for s in range(PASSES - e):
+                gather_scales(e, s, "gs%d_%d" % (e, s))
 
         def stationary(tile, s):
             if tile < ROUTED_TILES:
@@ -183,7 +187,8 @@ def tile_moe_shr_glu_silu_kernel(
 
         def quantised(first_tile, pair_banks):
             width = len(pair_banks) * PAIR
-            grouped = keep.tile([P, PACK * width], BF16, name="grouped%d" % first_tile, align_bytes=64)
+            name = "grouped%d" % first_tile
+            grouped = keep.tile([P, PACK * width], BF16, name=name, tag=name, align_bytes=64)
             for n, bank in enumerate(pair_banks):
                 turned = bank[:].rearrange("p (j u t) -> p j u t", j=2, u=2)
                 for j in range(2):
@@ -226,13 +231,20 @@ def tile_moe_shr_glu_silu_kernel(
                     op=MULT,
                 )
 
-        def finish(first_tile, codes, block_banks):
+        def finish(first_tile, codes, blocks, block_banks, aside=False):
             first = (first_tile - ROUTED_TILES) * P
             width = codes[0].shape[1]
-            for b, bank in enumerate(block_banks):
-                second_layer(bank[:, 0:width], SHARED, b, codes)
+            for b, bank in zip(blocks, block_banks):
+                ys = bank[:, 0:width]
+                second_layer(ys, SHARED, b, codes)
+                if aside:
+                    ys_sb = keep.tile([P, width], F32, name="ys_sb")
+                    nc.scalar.copy(out=ys_sb[:], in_=ys)
+                    ys = ys_sb[:]
                 result = work.tile([P, width], F32, name="result", tag="result", bufs=3 * BLOCKS)
-                nc.vector.tensor_tensor(out=result[:], in0=bank[:, 0:width], in1=windows[b][:, first:first + width], op=ADD)
+                (nc.gpsimd if aside else nc.vector).tensor_tensor(
+                    out=result[:], in0=ys, in1=windows[b][:, first:first + width], op=ADD
+                )
                 nc.sync.dma_start(out=out[b * P:(b + 1) * P, first:first + width], in_=result[:])
 
         spare, other_spare = banks[SPARE_BANKS[0]], banks[SPARE_BANKS[1]]
@@ -257,11 +269,13 @@ def tile_moe_shr_glu_silu_kernel(
         for tile in (0, 1):
             w3_side(tile)
 
-        for b, (tag, engine) in enumerate((("w1_0", nc.gpsimd), ("w1s_first", nc.gpsimd), ("w3_0", nc.vector))):
-            windows.append(keep.tile([P, T], F32, name="window%d" % b, tag=tag, align_bytes=64))
-            engine.memset(windows[b][:].bitcast(I32), 0)
-
+        gather_scales(1, PASSES - 1, "w3_0")
         codes_0 = quantised(0, [spare])
+
+        for b, tag in enumerate(("w1_0", "w1s_first", "grouped0")):
+            windows.append(keep.tile([P, T], F32, name="window%d" % b, tag=tag, align_bytes=64))
+            nc.gpsimd.memset(windows[b][:].bitcast(I32), 0)
+
         w1_side(2)
         scatter(0, [0, 1], codes_0, other_spare)
         w1_side(3)
@@ -281,11 +295,13 @@ def tile_moe_shr_glu_silu_kernel(
         first_layer(8)
         codes_4_to_7 = quantised(4, [spare, other_spare])
         scatter(1, [2], codes_1, w1_bank(8))
-        for tile in (9, 10, 11):
-            first_layer(tile)
+        first_layer(9)
+        first_layer(10)
 
-        finish(4, codes_4_to_7, [other_spare, spare, w1_bank(10)])
+        finish(4, codes_4_to_7, [0], [other_spare], aside=True)
+        first_layer(11)
+        finish(4, codes_4_to_7, [1, 2], [spare, w1_bank(10)])
         codes_8_9 = quantised(8, [w3_bank(8)])
         codes_10_11 = quantised(10, [w1_bank(11)])
-        finish(8, codes_8_9, [w3_bank(9), w3_bank(10), other_spare])
-        finish(10, codes_10_11, [w3_bank(11), spare, w1_bank(10)])
+        finish(8, codes_8_9, range(BLOCKS), [other_spare, spare, w3_bank(9)])
+        finish(10, codes_10_11, range(BLOCKS), [w1_bank(10), w3_bank(10), w3_bank(11)])

from contextlib import ExitStack

import concourse.mybir as mybir
from concourse.masks import make_identity

K, T, E, C, H, N = 1536, 1024, 2, 256, 512, 384
FLOPS = 2 * (T + E * C) * (2 * K * H + H * N)

F32 = mybir.dt.float32
BF16 = mybir.dt.bfloat16
I32 = mybir.dt.int32
U32 = mybir.dt.uint32
U16 = mybir.dt.uint16
U8 = mybir.dt.uint8
FP8X4 = mybir.dt.float8_e4m3fn_x4
FP4X4 = mybir.dt.float4_e2m1fn_x4
MULT = mybir.AluOpType.mult
ADD = mybir.AluOpType.add
SILU = mybir.ActivationFunctionType.Silu

P = 128
PACK = 4
PASSES = K // (P * PACK)
SHARED = E
BLOCKS = N // P
PER_COLUMN = 16
PAIR = 2 * P
ROUTED_TILES = E * C // P
TILES = ROUTED_TILES + T // P
W1, W3 = 0, 1
W1_BANKS = (0, 1)
W3_BANKS = (2, 3, 4, 6)
SPARE_BANKS = (5, 7)
WARM_UPS = 3


def tile_moe_shr_glu_silu_kernel(
    tc, x_words, x_scales, w1_words, w1_scales, w3_words, w3_scales, w2_words, w2_scales, gate, offs, out
):
    nc = tc.nc
    with ExitStack() as ctx:
        keep = ctx.enter_context(tc.tile_pool(name="keep", bufs=1))
        work = ctx.enter_context(tc.tile_pool(name="work", bufs=1))
        psum = ctx.enter_context(tc.psum_pool(name="psum", bufs=1))

        offsets = keep.tile([P, E * C // PER_COLUMN], U16, name="offsets")
        xw = [keep.tile([P, T], U32, name="xw%d" % s, align_bytes=64) for s in range(PASSES)]
        xs = keep.tile([P, PASSES, T], U8, name="xs", align_bytes=64)
        w1_head = keep.tile([P, 1, 2 * H], U8, name="w1_head", align_bytes=64)
        w1 = [
            keep.tile([P, PASSES - (e == 0), 2 * H], U8, name="w1_%d" % e, tag="w1_%d" % e, align_bytes=64)
            for e in range(E + 1)
        ]
        w3 = [keep.tile([P, PASSES, 2 * H], U8, name="w3_%d" % e, tag="w3_%d" % e, align_bytes=64) for e in range(E + 1)]
        w2 = keep.tile([P, E + 1, 2 * N], U8, name="w2", align_bytes=64)
        w1s_first = keep.tile([P, PASSES, H], U8, name="w1s_first", tag="w1s_first", align_bytes=64)
        w1s_rest = keep.tile([P, E * PASSES, H], U8, name="w1s_rest", align_bytes=64)
        w3s_first = keep.tile([P, PASSES, H], U8, name="w3s_first", align_bytes=64)
        w3s_rest = keep.tile([P, E * PASSES, H], U8, name="w3s_rest", align_bytes=64)
        w2s = keep.tile([P, E + 1, N], U8, name="w2s", align_bytes=64)
        gate_sb = keep.tile([P, E * C], F32, name="gate_sb")
        ident = keep.tile([P, P], F32, name="ident")
        banks = [psum.tile([P, H], F32, name="bank%d" % i) for i in range(8)]

        def load_scales(plane, rows, quarters=range(4)):
            for r in quarters:
                nc.sync.dma_start(
                    out=plane[r:P:32].bitcast(I32), in_=rows[:, r:16:4, :].rearrange("s q c -> q s c").bitcast(I32)
                )

        def load_x(s):
            nc.sync.dma_start(out=xw[s][:].bitcast(I32), in_=x_words[s].rearrange("p t r -> p (t r)").bitcast(I32))

        def load_w(tile, words):
            nc.sync.dma_start(out=tile[:].bitcast(I32), in_=words.rearrange("s p c -> p s c").bitcast(I32))

        def by_pass(packed):
            return packed.rearrange("e s p c -> (e s) p c")

        nc.gpsimd.memset(w1s_first[:].bitcast(I32), 0)
        for plane in (xs, w3s_first, w1s_rest, w3s_rest, w2s):
            nc.vector.memset(plane[:].bitcast(I32), 0)
        make_identity(nc, ident[:])

        nc.sync.dma_start(offsets[:], offs)
        load_x(0)
        load_x(1)
        load_scales(w1s_first, w1_scales[0])
        load_x(2)
        load_w(w1_head, w1_words[0, 0:1])
        load_scales(xs, x_scales)
        load_w(w1[0], w1_words[0, 1:PASSES])
        load_w(w3[0], w3_words[0])
        load_scales(w3s_first, w3_scales[0])
        load_w(w2, by_pass(w2_words))
        load_scales(w2s, by_pass(w2_scales), range(3))
        load_w(w1[1], w1_words[1])
        load_scales(w1s_rest, by_pass(w1_scales[1:E + 1]))
        load_scales(w2s, by_pass(w2_scales), [3])
        nc.sync.dma_start(out=gate_sb[:], in_=gate[0:P, :])
        load_w(w3[1], w3_words[1])
        load_scales(w3s_rest, by_pass(w3_scales[1:E + 1]))
        load_w(w1[SHARED], w1_words[SHARED])
        load_w(w3[SHARED], w3_words[SHARED])

        def slots(e):
            return offsets[:, e * C // PER_COLUMN:(e + 1) * C // PER_COLUMN]

        slot_words = []
        for s in range(PASSES):
            gw = keep.tile([P, E * C], U32, name="gw%d" % s, align_bytes=64)
            nc.vector.tensor_copy(out=gw[:], in_=xw[s][:].indirect(offsets[:]))
            slot_words.append(gw)
        slot_scales = {}

        def gather_scales(e, s, tag):
            slot_scales[e, s] = keep.tile([P, C], U8, name="gs%d_%d" % (e, s), tag=tag, align_bytes=64)
            nc.vector.tensor_copy(out=slot_scales[e, s][:], in_=xs[:, s, :].indirect(slots(e)))

        for e in range(E):
            for s in range(PASSES - e):
                gather_scales(e, s, "gs%d_%d" % (e, s))

        def stationary(tile, s):
            if tile < ROUTED_TILES:
                e, place = divmod(tile * P, C)
                return e, slot_words[s][:, tile * P:(tile + 1) * P], slot_scales[e, s][:, place:place + P]
            cols = slice((tile - ROUTED_TILES) * P, (tile - ROUTED_TILES + 1) * P)
            return SHARED, xw[s][:, cols], xs[:, s, cols]

        def moving(matrix, e, s):
            if e > 0:
                return (w1, w3)[matrix][e][:, s, :], (w1s_rest, w3s_rest)[matrix][:, (e - 1) * PASSES + s, :]
            if matrix == W3:
                return w3[0][:, s, :], w3s_first[:, s, :]
            return (w1_head[:, 0, :] if s == 0 else w1[0][:, s - 1, :]), w1s_first[:, s, :]

        def w1_bank(tile):
            return banks[W1_BANKS[tile % len(W1_BANKS)]]

        def w3_bank(tile):
            return banks[W3_BANKS[tile % len(W3_BANKS)]]

        def first_layer_pass(bank, tile, matrix, s):
            e, words, scales = stationary(tile, s)
            weights, plane = moving(matrix, e, s)
            nc.tensor.matmul_mx(
                out=bank[:],
                lhsT=words.bitcast(FP8X4),
                lhsT_scale=scales,
                rhs=weights.bitcast(FP4X4),
                rhs_scale=plane,
                start=(s == 0),
                stop=(s == PASSES - 1),
            )

        acts = {}
        hidden = {}

        def silu(tile):
            acts[tile] = work.tile([P, H], F32, name="act", tag="act", bufs=TILES)
            nc.scalar.activation(
                out=acts[tile][:].rearrange("t (u p v) -> t u p v", u=2, v=2),
                in_=w1_bank(tile)[:].rearrange("t (p u v) -> t u p v", u=2, v=2),
                func=SILU,
            )

        def w1_side(tile):
            for s in range(PASSES):
                first_layer_pass(w1_bank(tile), tile, W1, s)
            silu(tile)

        def w3_side(tile):
            for s in range(PASSES):
                first_layer_pass(w3_bank(tile), tile, W3, s)
            hidden[tile] = work.tile([P, H], BF16, name="h", tag="h", bufs=TILES, align_bytes=64)
            nc.vector.tensor_tensor(
                out=hidden[tile][:].rearrange("t (u p v) -> t u p v", u=2, v=2),
                in0=w3_bank(tile)[:].rearrange("t (p u v) -> t u p v", u=2, v=2),
                in1=acts[tile][:].rearrange("t (u p v) -> t u p v", u=2, v=2),
                op=MULT,
            )

        def first_layer(tile):
            w1_side(tile)
            w3_side(tile)

        def quantised(first_tile, pair_banks):
            width = len(pair_banks) * PAIR
            name = "grouped%d" % first_tile
            grouped = keep.tile([P, PACK * width], BF16, name=name, tag=name, align_bytes=64)
            for n, bank in enumerate(pair_banks):
                turned = bank[:].rearrange("p (j u t) -> p j u t", j=2, u=2)
                for j in range(2):
                    pairs = hidden[first_tile + 2 * n + j][:].bitcast(F32)
                    for u in range(2):
                        nc.tensor.transpose(turned[:, j, u, :], pairs[:, u * P:(u + 1) * P], ident[:])
                nc.scalar.copy(
                    out=grouped[:, n * PACK * PAIR:(n + 1) * PACK * PAIR].bitcast(F32).rearrange("p (j t u) -> p j t u", j=2, u=2),
                    in_=turned.rearrange("p j u t -> p j t u"),
                )
            hw = keep.tile([P, width], U32, name="hw%d" % first_tile, align_bytes=64)
            hs = keep.tile([P, width], U8, name="hs%d" % first_tile, align_bytes=64)
            nc.vector.quantize_mx(out=hw[:].bitcast(FP8X4), scales=hs[:], in_=grouped[:])
            return hw, hs

        def second_layer(y, e, b, codes):
            hw, hs = codes
            nc.tensor.matmul_mx(
                out=y,
                lhsT=w2[:, e, 2 * b * P:2 * (b + 1) * P].bitcast(FP4X4),
                lhsT_scale=w2s[:, e, b * P:(b + 1) * P],
                rhs=hw[:].bitcast(FP8X4),
                rhs_scale=hs[:],
                start=True,
                stop=True,
            )

        windows = []

        def scatter(e, blocks, codes, bank):
            for n, b in enumerate(blocks):
                second_layer(bank[:, n * C:(n + 1) * C], e, b, codes)
            y_sb = work.tile([P, len(blocks) * C], F32, name="y_sb", tag="y_sb", bufs=E * BLOCKS - 1)
            nc.scalar.copy(out=y_sb[:], in_=bank[:, 0:len(blocks) * C])
            for n, b in enumerate(blocks):
                nc.vector.tensor_tensor(
                    out=windows[b][:].indirect(slots(e)),
                    in0=y_sb[:, n * C:(n + 1) * C],
                    in1=gate_sb[:, e * C:(e + 1) * C],
                    op=MULT,
                )

        def finish(first_tile, codes, blocks, block_banks, aside=False):
            first = (first_tile - ROUTED_TILES) * P
            width = codes[0].shape[1]
            for b, bank in zip(blocks, block_banks):
                ys = bank[:, 0:width]
                second_layer(ys, SHARED, b, codes)
                if aside:
                    ys_sb = keep.tile([P, width], F32, name="ys_sb")
                    nc.scalar.copy(out=ys_sb[:], in_=ys)
                    ys = ys_sb[:]
                result = work.tile([P, width], F32, name="result", tag="result", bufs=3 * BLOCKS)
                (nc.gpsimd if aside else nc.vector).tensor_tensor(
                    out=result[:], in0=ys, in1=windows[b][:, first:first + width], op=ADD
                )
                nc.sync.dma_start(out=out[b * P:(b + 1) * P, first:first + width], in_=result[:])

        spare, other_spare = banks[SPARE_BANKS[0]], banks[SPARE_BANKS[1]]

        head_words, head_plane = moving(W1, 0, 0)
        for warm_up in range(WARM_UPS):
            nc.tensor.matmul_mx(
                out=other_spare[:],
                lhsT=slot_words[0][:, 0:P].bitcast(FP8X4),
                lhsT_scale=head_plane[:, 0:P],
                rhs=head_words.bitcast(FP4X4),
                rhs_scale=head_plane,
                start=True,
                stop=True,
            )

        for s in range(PASSES):
            for tile in (0, 1):
                first_layer_pass(w1_bank(tile), tile, W1, s)
        for tile in (0, 1):
            silu(tile)
        for tile in (0, 1):
            w3_side(tile)

        gather_scales(1, PASSES - 1, "w3_0")
        codes_0 = quantised(0, [spare])

        for b, tag in enumerate(("w1_0", "w1s_first", "grouped0")):
            windows.append(keep.tile([P, T], F32, name="window%d" % b, tag=tag, align_bytes=64))
            nc.gpsimd.memset(windows[b][:].bitcast(I32), 0)

        w1_side(2)
        scatter(0, [0, 1], codes_0, other_spare)
        w1_side(3)
        w3_side(2)
        w3_side(3)

        w1_side(4)
        w1_side(5)
        scatter(0, [2], codes_0, w1_bank(4))
        w3_side(4)
        w3_side(5)
        codes_1 = quantised(2, [w1_bank(5)])
        first_layer(6)
        scatter(1, [0], codes_1, w1_bank(6))
        first_layer(7)
        scatter(1, [1], codes_1, w1_bank(7))
        first_layer(8)
        codes_4_to_7 = quantised(4, [spare, other_spare])
        scatter(1, [2], codes_1, w1_bank(8))
        first_layer(9)
        first_layer(10)

        finish(4, codes_4_to_7, [0], [other_spare], aside=True)
        first_layer(11)
        finish(4, codes_4_to_7, [1, 2], [spare, w1_bank(10)])
        codes_8_9 = quantised(8, [w3_bank(8)])
        codes_10_11 = quantised(10, [w1_bank(11)])
        finish(8, codes_8_9, range(BLOCKS), [other_spare, spare, w3_bank(9)])
        finish(10, codes_10_11, range(BLOCKS), [w1_bank(10), w3_bank(10), w3_bank(11)])
